import numpy as np
CORES = [24,26,29,31,48,50,53,55]
N = 8
J, Q = 512, 2048
def entries(a): return a.T.reshape(-1)
def pack(v, P): return np.ascontiguousarray(np.asarray(v, np.int32).reshape(-1, P).T)
def split(rng, total, parts):
    c = np.sort(rng.integers(0, total + 1, parts - 1)); return np.diff(np.concatenate([[0], c, [total]]))
def lists(rng, how):
    s = np.concatenate([[0], rng.integers(1 - Q // 2, Q // 2 + 1, N - 1), [int(rng.integers(1 - Q // 2, 1))]])
    if how == "early": s[1:] = -Q; s[N] = -2 * Q
    if how == "late": s[1:] = Q; s[N] = 0
    if how == "long":
        z = int(rng.integers(1, N - 1)); s[1:z] = -rng.integers(1, Q, z - 1); s[z] = -Q; s[z + 1] = Q; s[z + 2:N] = rng.integers(1, Q, N - z - 2); s[N] = -int(rng.integers(0, Q - s[N - 1] + 1))
    if how == "sway":
        z = int(rng.integers(1, N - 2)); e = int(rng.integers(z + 1, N - 1)); s[1:] = -rng.integers(Q // 2 + 1, Q, N); s[z + 1:e + 1] = rng.integers(Q // 2 + 1, Q - 1, e - z); s[e + 1] = s[e] - Q; s[N] = s[N - 1] - Q + int(rng.integers(1, -s[N - 1]))
    tot = Q + np.diff(s)
    L = np.stack([split(rng, int(t), J) for t in tot])
    if how == "gaps":
        L = np.zeros((N, J), np.int64)
        for r in range(N): m = 1 if r & 1 else 8; L[r, 1 + rng.permutation(J - 2)[:m]] = split(rng, int(tot[r]), m)
    if how == "long":
        L = np.zeros((N, J), np.int64); L[np.arange(N), rng.integers(0, J, N)] = tot
    return {"ln": np.stack([pack(l, 16) for l in L])}
def setup_inputs(rng):
    return dict({"x": rng.standard_normal((N, 128, J), dtype=np.float32)}, **lists(rng, "uniform"))
def setup_inputs_early(rng):
    d = setup_inputs(rng); d.update(lists(rng, "early"))
    for k in ("x",): d[k] = (d[k].astype(np.float32) * 1048576.0).astype(d[k].dtype)
    return d
def setup_inputs_gaps(rng):
    d = setup_inputs(rng); d.update(lists(rng, "gaps"))
    for k in ("x",): d[k] = (d[k].astype(np.float32) * (1 / 1024.0)).astype(d[k].dtype)
    return d
def setup_inputs_late(rng):
    d = setup_inputs(rng); d.update(lists(rng, "late"))
    return d
def setup_inputs_long(rng):
    d = setup_inputs(rng); d.update(lists(rng, "long"))
    return d
def setup_inputs_sway(rng):
    d = setup_inputs(rng); d.update(lists(rng, "sway"))
    return d
def check_inputs(x):
    bad = []
    if x["ln"].min() < 0 or x["ln"].max() >= N * Q + 1: bad.append("ln out of range")
    if int(x["ln"].sum()) > N * Q: bad.append("the lengths come to more than N * Q")
    c = np.concatenate([[0], np.cumsum([int(a.sum()) for a in x["ln"]])])
    if any(c[r] < (r - 1) * Q or c[r + 1] > (r + 2) * Q for r in range(N)): bad.append("the sums of the lengths before or up to a rank leave their bounds")
    return bad
def reference(x, ln):
    got = np.concatenate([np.repeat(x[r], entries(ln[r]), axis=1) for r in range(N)], axis=1)[:, :N * Q]
    Y = np.zeros((128, N * Q), x.dtype); Y[:, :got.shape[1]] = got
    return {"y": np.stack([Y[:, Q * r:Q * r + Q] for r in range(N)])}

@@ -1,0 +1,335 @@
+from concourse.bass import DstId, RemoteDMATransfer
+from concourse.mybir import AluOpType, ActivationFunctionType, AxisListType
+
+NEV = 64
+SCRATCH = {
+    "Li": ("sbuf", [128, 32], "int32"),
+    "fwi": ("sbuf", [128, 16], "int32"),
+    "fwf": ("sbuf", [128, 16], "float32"),
+    "rs": ("sbuf", [128, 4], "float32"),
+    "Lf": ("sbuf", [128, 32], "float32"),
+    "Sc": ("sbuf", [128, 36], "float32"),
+    "SB": ("sbuf", [128, 16], "float32"),
+    "zz": ("sbuf", [128, 32], "float32"),
+    "kc": ("sbuf", [128, 16], "float32"),
+    "ni": ("sbuf", [128, 128], "int32"),
+    "pi": ("sbuf", [128, 4], "int32"),
+    "pj": ("sbuf", [128, 4], "int32"),
+    "pf": ("sbuf", [128, 4], "float32"),
+    "am": ("sbuf", [128, 128], "int32"),
+    "bm": ("sbuf", [128, 128], "int32"),
+    "lm": ("sbuf", [128, 64], "int32"),
+    "Aeq": ("sbuf", [128, 128], "float32"),
+    "Alt": ("sbuf", [128, 128], "float32"),
+    "Agt": ("sbuf", [128, 128], "float32"),
+    "Ang": ("sbuf", [128, 128], "float32"),
+    "Ab": ("sbuf", [128, 128], "float32"),
+    "ones": ("sbuf", [128, 128], "float32"),
+    "one16": ("sbuf", [128, 128], "float16"),
+    "nb": ("sbuf", [128, 128], "bfloat16"),
+    "lt": ("sbuf", [128, 64], "bfloat16"),
+    "t1": ("sbuf", [128, 128], "float16"),
+    "t2": ("sbuf", [128, 128], "float16"),
+    "hI": ("sbuf", [128, 128], "float16"),
+    "UU": ("sbuf", [128, 128], "float16"),
+    "ci": ("sbuf", [128, 12], "int32"),
+    "hl": ("sbuf", [128, 24], "int32"),
+    "hlf": ("sbuf", [128, 24], "float32"),
+    "oh": ("sbuf", [128, 1536], "bfloat16"),
+    "sg": ("sbuf", [128, 768], "bfloat16"),
+    "GL": ("sbuf", [128, 128], "float16"),
+    "R2": ("sbuf", [128, 128], "float16"),
+    "osb": ("sbuf", [128, 2], "uint16"),
+    "off": ("sbuf", [128, 128], "uint16"),
+    "xw": ("sbuf", [128, 1540], "float32"),
+    "rl": ("sbuf", [128, 256], "float32"),
+    "yt": ("sbuf", [128, 2048], "float32"),
+    "cps": ("psum", [128, 512], "float32"),
+    "bps": ("psum", [128, 512], "float32"),
+    "gps": ("psum", [128, 512], "float32"),
+    "fps": ("psum", [128, 512], "float32"),
+}
+SEMAPHORES = (["lnld", "xld", "yst", "ysc", "sent", "fw", "xm", "xp", "xq", "rla"] + ["l%d" % k for k in range(8)]
+              + ["e%d" % k for k in range(NEV)])
+
+
+def bits(mask):
+    return [b for b in range(32) if (mask >> b) & 1]
+
+
+def tomask(bs):
+    m = 0
+    for b in bs:
+        m |= 1 << b
+    return m
+
+
+def route(T, topo):
+    C = T.cores
+    n = len(C)
+    cut = [r for r in range(n - 1) if topo.chip(C[r]) != topo.chip(C[r + 1])]
+    assert len(cut) == 1
+    b = cut[0]
+    first, second = list(range(b + 1)), list(range(b + 1, n))
+    assert topo.may_write(C[b], C[b + 1])
+    fwd = [r for r in first if r != b and all(topo.may_write(C[r], C[q]) for q in second)][0]
+    cand = [r for r in second if r != b + 1 and topo.may_write(C[r], C[b])]
+    near = [r for r in cand if r == b + 2][0]
+    far = [r for r in cand if topo.die(C[r]) != topo.die(C[near])][0]
+    return b, first, second, fwd, near, far
+
+
+def rank_program(g, core, T, topo):
+    r = T.rank_of(core)
+    if r is None:
+        return
+    C = T.cores
+    n = len(C)
+    b, first, second, fwd, near, far = route(T, topo)
+    mine = first if r in first else second
+    A = AluOpType
+    AF = ActivationFunctionType
+    V, S, P, Y = g.vector, g.scalar, g.tensor, g.sync
+    cnt = [0]
+    sent = [0]
+
+    def ev(*ins):
+        s = T.sem["e%d" % cnt[0]]
+        cnt[0] += 1
+        for i in ins:
+            i.then_inc(s, 1)
+        return (s, len(ins))
+
+    def wt(q, *toks):
+        for s, v in toks:
+            q.wait_ge(s, v)
+
+    onchip = bits(topo.mask(C[mine[0]], C[mine[1]]))
+    offchip = bits(topo.mask(C[b], C[b + 1]))
+    hi8 = [e for e in onchip if e not in offchip]
+    ev8, od8 = onchip[0::2], onchip[1::2]
+
+    def tr(src, dst, sem, ranks, engines):
+        ids = [DstId(rid=topo.addr(C[q])[0], pnc=topo.addr(C[q])[1]) for q in ranks]
+        sent[0] += len(engines)
+        return RemoteDMATransfer(dst_ids=ids, dma_engine_mask=tomask(engines), remote_sem=sem, srcs=[src],
+                                 dsts=list(dst))
+
+    def send(*trs):
+        g.remote_dma_fused(list(trs), local_sem=T.sem.sent)
+
+    def slot(k, q):
+        return 512 * (k - q + 1)
+
+    lists = [k for k in (r - 1, r, r + 1) if 0 <= k < n]
+    nc = 4 * len(lists)
+    w0 = slot(lists[0], r)
+    w1 = slot(lists[-1], r) + 512
+    NL = len(offchip)
+
+    def ldests(k):
+        grp = first if k in first else second
+        d = [q for q in grp if q != k and (q >= k - 1 or (k in first and q == fwd))]
+        if k == b:
+            d.append(b + 1)
+        return d
+
+    Y.dma_start(T.Li[:, 4 * r:4 * r + 4], T.ln[:]).then_inc(T.sem.lnld, 16)
+    xs = slot(r, r)
+    S.dma_start(T.xw[:, xs:xs + 512], T.x[:]).then_inc(T.sem.xld, 16)
+
+    e_p = ev(g.iota(T.pi[:, 0:1], [[0, 1]], 0, 1))
+    e_n = ev(g.iota(T.ni[:], [[1, 128]], 0, 0))
+
+    g.wait_ge(T.sem.lnld, 16)
+    ld = ldests(r)
+    send(tr(T.Li[:, 4 * r:4 * r + 4], [T.Li[:, 4 * r:4 * r + 4] for q in ld], T.sem["l%d" % r], ld, offchip))
+
+    g.wait_ge(T.sem.xld, 16)
+    xall = T.xw[:, xs:xs + 512]
+
+    def xdst(q):
+        s = slot(r, q)
+        return T.xw[:, s:s + 512]
+
+    def xsend(k):
+        if k == b:
+            return [(b + 1, offchip), (k - 1, hi8)]
+        if k == b + 1:
+            return []
+        q2 = [q for q in (k - 1, k + 1) if 0 <= q < n]
+        pool = hi8 if k in (fwd, near, far) else onchip
+        if len(q2) == 1:
+            return [(q2[0], pool)]
+        return [(q2[0], pool[0::2]), (q2[1], pool[1::2])]
+
+    nx = {}
+    for k in range(n):
+        for q, e in xsend(k):
+            nx[(k, q)] = len(e)
+    if r == b + 1:
+        s = slot(r, near)
+        send(tr(T.xw[:, xs:xs + 256], [T.xw[:, s:s + 256]], T.sem.xm, [near], od8),
+             tr(T.xw[:, xs + 256:xs + 512], [T.rl[:]], T.sem.rla, [far], ev8))
+        send(tr(T.xw[:, xs + 256:xs + 512], [T.xw[:, s + 256:s + 512]], T.sem.xq, [near], od8))
+    else:
+        send(*[tr(xall, [xdst(q)], T.sem.xm if q > r else T.sem.xp, [q], e) for q, e in xsend(r)])
+
+    if r == fwd:
+        for k in first:
+            if k != r:
+                g.wait_ge(T.sem["l%d" % k], NL)
+        m = 4 * len(first)
+        send(tr(T.Li[:, 0:m], [T.fwi[:, 0:m] for q in second], T.sem.fw, second, offchip))
+    if r == far:
+        k = b + 1
+        g.wait_ge(T.sem["l%d" % k], NL)
+        send(tr(T.Li[:, 4 * k:4 * k + 4], [T.Li[:, 4 * k:4 * k + 4]], T.sem["l%d" % k], [b], offchip))
+        g.wait_ge(T.sem.rla, len(ev8))
+        s = slot(k, b)
+        send(tr(T.rl[:], [T.xw[:, s + 256:s + 512]], T.sem.xq, [b], offchip))
+    if r == near:
+        k = b + 1
+        g.wait_ge(T.sem.xm, len(od8))
+        s, s0 = slot(k, b), slot(k, r)
+        send(tr(T.xw[:, s0:s0 + 256], [T.xw[:, s:s + 256]], T.sem.xp, [b], offchip))
+
+    e_m = ev(V.memset(T.kc[:], float(-16 * r)), V.memset(T.ones[:], 1.0))
+    zero = [V.memset(T.Sc[:], 0.0), V.memset(T.zz[:], 0.0)]
+    if r >= n - 2:
+        zero.append(V.memset(T.xw[:, w1:w1 + 4], 0.0))
+        w1 += 1
+    e_z = ev(*zero)
+    wt(V, e_p, e_n)
+    e1 = ev(V.tensor_scalar(T.pj[:, 0:1], T.pi[:, 0:1], 7, None, A.bitwise_and),
+            V.tensor_scalar(T.pj[:, 1:2], T.pi[:, 0:1], 3, None, A.arith_shift_right),
+            V.tensor_scalar(T.pj[:, 2:3], T.pi[:, 0:1], 12, None, A.bitwise_and),
+            V.tensor_copy(T.pf[:, 3:4], T.pi[:, 0:1]),
+            V.tensor_scalar(T.am[:], T.ni[:], 7, None, A.bitwise_and),
+            V.tensor_scalar(T.bm[:], T.ni[:], 3, None, A.arith_shift_right),
+            V.tensor_scalar(T.lm[:], T.ni[:, 0:64], 15, None, A.bitwise_and))
+    i_nb = V.tensor_scalar(T.nb[:], T.ni[:], -1.0, None, A.mult)
+    wt(V, e1, e_z, e_m)
+    base_lists = [k for k in mine if k < lists[0] and not (r in second and k in first)]
+    scan_lists = base_lists + lists
+    e0 = 4 * len(base_lists)
+    e2 = ev(V.tensor_copy(T.pf[:, 0:2], T.pj[:, 0:2]),
+            V.tensor_scalar(T.osb[:, 0:1], T.pj[:, 2:3], float(e0), None, A.add))
+    e_t = ev(i_nb, V.tensor_scalar(T.lt[:], T.lm[:], 0.5, None, A.add))
+    wt(V, e2)
+    e3 = ev(V.tensor_scalar(T.Aeq[:], T.am[:], T.pf[:, 0:1], None, A.is_equal),
+            V.tensor_scalar(T.Ab[:], T.bm[:], T.pf[:, 1:2], -1.0, A.is_lt, A.mult))
+    e4 = ev(V.tensor_scalar(T.Alt[:], T.am[:], T.pf[:, 0:1], None, A.is_gt),
+            V.tensor_scalar(T.Agt[:], T.am[:], T.pf[:, 0:1], None, A.is_lt))
+    wt(V, e3)
+    e5 = ev(V.tensor_tensor(T.Ang[:], T.Ab[:], T.Aeq[:], A.mult))
+    e6 = ev(V.tensor_scalar(T.t1[:], T.ni[:], T.pf[:, 3:4], 0.5, A.is_ge, A.mult),
+            V.tensor_scalar(T.t2[:], T.ni[:], T.pf[:, 3:4], 0.5, A.is_gt, A.mult))
+    wt(V, e6)
+    e7 = ev(V.tensor_tensor(T.hI[:], T.t1[:], T.t2[:], A.subtract),
+            V.tensor_tensor(T.UU[:], T.t1[:], T.t2[:], A.add),
+            V.tensor_copy(T.one16[:], T.ones[:]))
+
+    wt(P, e_m)
+    P.matmul(T.cps[:, 0:nc], T.ones[:], T.kc[:, 0:nc], True, False)
+    k0, k1 = scan_lists[0], scan_lists[-1]
+    V.wait_ge(T.sem.lnld, 16)
+    for k in scan_lists:
+        if k != r:
+            V.wait_ge(T.sem["l%d" % k], NL)
+    ns = 4 * len(scan_lists)
+    e8 = ev(V.tensor_copy(T.Lf[:, 0:ns], T.Li[:, 4 * k0:4 * k1 + 4]))
+    wt(V, e8)
+    e9 = ev(V.tensor_tensor_scan(T.Sc[:, 1:1 + ns], T.zz[:, 0:ns], T.Lf[:, 0:ns], 0.0, A.add, A.add))
+    wt(V, e9)
+    e10 = ev(V.tensor_copy(T.SB[:], T.Sc[:].indirect(T.osb[:, 0:1])))
+    wt(P, e5, e8)
+    P.matmul(T.cps[:, 0:nc], T.Ang[:], T.Lf[:, e0:e0 + nc], False, False)
+    wt(P, e3, e9)
+    P.matmul(T.cps[:, 0:nc], T.Aeq[:], T.Sc[:, e0 + 1:e0 + 1 + nc], False, False)
+    wt(P, e4, e10)
+    P.matmul(T.cps[:, 0:nc], T.Alt[:], T.SB[:, 4:4 + nc], False, False)
+    e11 = ev(P.matmul(T.cps[:, 0:nc], T.Agt[:], T.SB[:, 0:nc], False, True))
+
+    if r in second:
+        nf = 4 * len([k for k in first if k < lists[0]])
+        V.wait_ge(T.sem.fw, NL)
+        f1 = ev(V.tensor_copy(T.fwf[:, 0:nf], T.fwi[:, 0:nf]))
+        wt(V, f1)
+        f2 = ev(V.tensor_reduce(T.rs[:, 0:1], T.fwf[:, 0:nf], AxisListType.X, A.add))
+        wt(P, f2)
+        f3 = ev(P.matmul(T.bps[:, 0:1], T.ones[:], T.rs[:, 0:1], True, True))
+        wt(V, e11, f3)
+        e12 = ev(V.tensor_scalar(T.ci[:, 0:nc], T.cps[:, 0:nc], T.bps[:, 0:1], 0.0, A.add, A.max))
+    else:
+        wt(V, e11)
+        e12 = ev(V.tensor_scalar(T.ci[:, 0:nc], T.cps[:, 0:nc], 0.0, None, A.max))
+    wt(V, e12)
+    e13 = ev(V.tensor_scalar(T.hl[:, 0:nc], T.ci[:, 0:nc], 4, None, A.arith_shift_right),
+             V.tensor_scalar(T.hl[:, nc:2 * nc], T.ci[:, 0:nc], 15, None, A.bitwise_and))
+    wt(V, e13)
+    e14 = ev(V.tensor_scalar(T.hlf[:, 0:2 * nc], T.hl[:, 0:2 * nc], -1.0, None, A.mult))
+    wt(V, e14, e_t)
+    wt(S, e14, e_t)
+
+    for t in range(0, nc, 2):
+        ins = []
+        for u in (t, t + 1):
+            ins.append(V.tensor_scalar(T.oh[:, 128 * u:128 * u + 128], T.nb[:], T.hlf[:, u:u + 1], None, A.is_equal))
+            ins.append(S.activation(T.sg[:, 64 * u:64 * u + 64], T.lt[:], AF.Sign, bias=T.hlf[:, nc + u:nc + u + 1],
+                                    scale=1.0))
+        wt(P, ev(*ins))
+        for u in (t, t + 1):
+            m = P.matmul(T.gps[:, 0:64], T.oh[:, 128 * u:128 * u + 128], T.sg[:, 64 * u:64 * u + 64], u == 0,
+                         u == nc - 1)
+    e15 = ev(m)
+    wt(V, e15, e7)
+    e16 = ev(V.tensor_copy(T.GL[:, 0:64], T.gps[:, 0:64]), V.tensor_copy(T.GL[:, 64:128], T.gps[:, 0:64]))
+    e17 = ev(V.tensor_scalar(T.R2[:], T.UU[:], T.gps[:, 15:16], None, A.mult))
+    wt(P, e7, e16)
+    P.matmul(T.fps[:, 0:128], T.GL[:], T.hI[:], True, False)
+    wt(P, e17)
+    e18 = ev(P.matmul(T.fps[:, 0:128], T.one16[:], T.R2[:], False, True))
+    wt(V, e18)
+    e19 = ev(V.tensor_copy(T.off[:], T.fps[:, 0:128]))
+
+    def arrived(q):
+        q.wait_ge(T.sem.xld, 16)
+        for k in lists:
+            if k == r:
+                continue
+            if k == b + 1 and r == near:
+                q.wait_ge(T.sem.xm, len(od8))
+                q.wait_ge(T.sem.xq, len(od8))
+            elif k == b + 1 and r == b:
+                q.wait_ge(T.sem.xp, len(offchip))
+                q.wait_ge(T.sem.xq, len(offchip))
+            elif k < r:
+                q.wait_ge(T.sem.xm, nx[(k, r)])
+            else:
+                q.wait_ge(T.sem.xp, nx[(k, r)])
+
+    arrived(V)
+    wt(V, e19)
+    arrived(S)
+    wt(S, e19, e_z)
+    win = T.xw[:, w0:w1]
+
+    def gat(q, c0, c1):
+        o = T.off[:, c0 // 16:c1 // 16]
+        if q is V:
+            return ev(V.tensor_copy(T.yt[:, c0:c1], win.indirect(o)))
+        return ev(S.activation(T.yt[:, c0:c1], win.indirect(o), AF.Copy))
+
+    g1 = gat(V, 0, 256)
+    g2 = gat(S, 256, 512)
+    g3 = gat(V, 512, 1280)
+    g4 = gat(S, 1280, 2048)
+    for tok, c0, c1 in ((g1, 0, 256), (g2, 256, 512), (g3, 512, 1280)):
+        wt(Y, tok)
+        Y.dma_start(T.y[:, c0:c1], T.yt[:, c0:c1]).then_inc(T.sem.yst, 16)
+    wt(S, g4)
+    S.dma_start(T.y[:, 1280:2048], T.yt[:, 1280:2048]).then_inc(T.sem.ysc, 16)
+    Y.wait_ge(T.sem.yst, 48)
+    S.wait_ge(T.sem.ysc, 16)
+    g.wait_ge(T.sem.sent, sent[0])

@@ -26,15 +26,15 @@ SCRATCH = {
     "Ab": ("sbuf", [128, 128], "float32"),
     "ones": ("sbuf", [128, 128], "float32"),
     "one16": ("sbuf", [128, 128], "float16"),
-    "nb": ("sbuf", [128, 128], "bfloat16"),
+    "nk": ("sbuf", [128, 128], "bfloat16"),
     "lt": ("sbuf", [128, 64], "bfloat16"),
     "t1": ("sbuf", [128, 128], "float16"),
     "t2": ("sbuf", [128, 128], "float16"),
-    "hI": ("sbuf", [128, 128], "float16"),
-    "UU": ("sbuf", [128, 128], "float16"),
-    "ci": ("sbuf", [128, 12], "int32"),
-    "hl": ("sbuf", [128, 24], "int32"),
-    "hlf": ("sbuf", [128, 24], "float32"),
+    "Dm": ("sbuf", [128, 128], "float16"),
+    "Am": ("sbuf", [128, 128], "float16"),
+    "hi": ("sbuf", [128, 12], "int32"),
+    "u": ("sbuf", [128, 12], "float32"),
+    "nv": ("sbuf", [128, 12], "float32"),
     "oh": ("sbuf", [128, 1536], "bfloat16"),
     "sg": ("sbuf", [128, 768], "bfloat16"),
     "GL": ("sbuf", [128, 128], "float16"),
@@ -49,7 +49,7 @@ SCRATCH = {
     "gps": ("psum", [128, 512], "float32"),
     "fps": ("psum", [128, 512], "float32"),
 }
-SEMAPHORES = (["lnld", "xld", "yst", "ysc", "sent", "fw", "xm", "xp", "xq", "rla"] + ["l%d" % k for k in range(8)]
+SEMAPHORES = (["lnld", "xld", "yst", "sent", "fw", "xm", "xp", "xq", "rla"] + ["l%d" % k for k in range(8)]
               + ["e%d" % k for k in range(NEV)])
 
 
@@ -132,7 +132,10 @@ def rank_program(g, core, T, topo):
         d = [q for q in grp if q != k and (q >= k - 1 or (k in first and q == fwd))]
         if k == b:
             d.append(b + 1)
-        return d
+        relay = fwd if k in first else far if k == b + 1 else k
+        if relay == k:
+            return [d]
+        return [[relay], [q for q in d if q != relay]]
 
     Y.dma_start(T.Li[:, 4 * r:4 * r + 4], T.ln[:]).then_inc(T.sem.lnld, 16)
     xs = slot(r, r)
@@ -142,8 +145,8 @@ def rank_program(g, core, T, topo):
     e_n = ev(g.iota(T.ni[:], [[1, 128]], 0, 0))
 
     g.wait_ge(T.sem.lnld, 16)
-    ld = ldests(r)
-    send(tr(T.Li[:, 4 * r:4 * r + 4], [T.Li[:, 4 * r:4 * r + 4] for q in ld], T.sem["l%d" % r], ld, offchip))
+    for ld in ldests(r):
+        send(tr(T.Li[:, 4 * r:4 * r + 4], [T.Li[:, 4 * r:4 * r + 4] for q in ld], T.sem["l%d" % r], ld, offchip))
 
     g.wait_ge(T.sem.xld, 16)
     xall = T.xw[:, xs:xs + 512]
@@ -194,7 +197,8 @@ def rank_program(g, core, T, topo):
         s, s0 = slot(k, b), slot(k, r)
         send(tr(T.xw[:, s0:s0 + 256], [T.xw[:, s:s + 256]], T.sem.xp, [b], offchip))
 
-    e_m = ev(V.memset(T.kc[:], float(-16 * r)), V.memset(T.ones[:], 1.0))
+    LOW = -15.0 / 32
+    e_m = ev(V.memset(T.kc[:], (LOW - 128 * r) / 8), V.memset(T.ones[:], 1.0 / 16))
     zero = [V.memset(T.Sc[:], 0.0), V.memset(T.zz[:], 0.0)]
     if r >= n - 2:
         zero.append(V.memset(T.xw[:, w1:w1 + 4], 0.0))
@@ -205,30 +209,31 @@ def rank_program(g, core, T, topo):
             V.tensor_scalar(T.pj[:, 1:2], T.pi[:, 0:1], 3, None, A.arith_shift_right),
             V.tensor_scalar(T.pj[:, 2:3], T.pi[:, 0:1], 12, None, A.bitwise_and),
             V.tensor_copy(T.pf[:, 3:4], T.pi[:, 0:1]),
+            V.tensor_scalar(T.pf[:, 2:3], T.pi[:, 0:1], 1.0, None, A.add),
             V.tensor_scalar(T.am[:], T.ni[:], 7, None, A.bitwise_and),
             V.tensor_scalar(T.bm[:], T.ni[:], 3, None, A.arith_shift_right),
             V.tensor_scalar(T.lm[:], T.ni[:, 0:64], 15, None, A.bitwise_and))
-    i_nb = V.tensor_scalar(T.nb[:], T.ni[:], -1.0, None, A.mult)
+    i_nk = V.tensor_scalar(T.nk[:], T.ni[:], 0.5, None, A.add)
     wt(V, e1, e_z, e_m)
     base_lists = [k for k in mine if k < lists[0] and not (r in second and k in first)]
     scan_lists = base_lists + lists
     e0 = 4 * len(base_lists)
     e2 = ev(V.tensor_copy(T.pf[:, 0:2], T.pj[:, 0:2]),
             V.tensor_scalar(T.osb[:, 0:1], T.pj[:, 2:3], float(e0), None, A.add))
-    e_t = ev(i_nb, V.tensor_scalar(T.lt[:], T.lm[:], 0.5, None, A.add))
+    e_t = ev(i_nk, V.tensor_scalar(T.lt[:], T.lm[:], -7.0, 1.0 / 16, A.add, A.mult))
     wt(V, e2)
-    e3 = ev(V.tensor_scalar(T.Aeq[:], T.am[:], T.pf[:, 0:1], None, A.is_equal),
+    e3 = ev(V.tensor_scalar(T.Aeq[:], T.am[:], T.pf[:, 0:1], 1.0 / 16, A.is_equal, A.mult),
             V.tensor_scalar(T.Ab[:], T.bm[:], T.pf[:, 1:2], -1.0, A.is_lt, A.mult))
-    e4 = ev(V.tensor_scalar(T.Alt[:], T.am[:], T.pf[:, 0:1], None, A.is_gt),
-            V.tensor_scalar(T.Agt[:], T.am[:], T.pf[:, 0:1], None, A.is_lt))
+    e4 = ev(V.tensor_scalar(T.Alt[:], T.am[:], T.pf[:, 0:1], 1.0 / 16, A.is_gt, A.mult),
+            V.tensor_scalar(T.Agt[:], T.am[:], T.pf[:, 0:1], 1.0 / 16, A.is_lt, A.mult))
     wt(V, e3)
     e5 = ev(V.tensor_tensor(T.Ang[:], T.Ab[:], T.Aeq[:], A.mult))
-    e6 = ev(V.tensor_scalar(T.t1[:], T.ni[:], T.pf[:, 3:4], 0.5, A.is_ge, A.mult),
-            V.tensor_scalar(T.t2[:], T.ni[:], T.pf[:, 3:4], 0.5, A.is_gt, A.mult))
+    e6 = ev(V.tensor_scalar(T.t1[:], T.ni[:], T.pf[:, 3:4], 0.5, A.is_equal, A.mult),
+            V.tensor_scalar(T.t2[:], T.ni[:], T.pf[:, 2:3], 0.5, A.is_equal, A.mult))
     wt(V, e6)
-    e7 = ev(V.tensor_tensor(T.hI[:], T.t1[:], T.t2[:], A.subtract),
-            V.tensor_tensor(T.UU[:], T.t1[:], T.t2[:], A.add),
-            V.tensor_copy(T.one16[:], T.ones[:]))
+    e7 = ev(V.tensor_tensor(T.Dm[:], T.t1[:], T.t2[:], A.subtract),
+            V.tensor_tensor(T.Am[:], T.t1[:], T.t2[:], A.add),
+            V.memset(T.zz[:], 0.0) if False else V.tensor_scalar(T.one16[:], T.ones[:], 16.0, None, A.mult))
 
     wt(P, e_m)
     P.matmul(T.cps[:, 0:nc], T.ones[:], T.kc[:, 0:nc], True, False)
@@ -260,34 +265,32 @@ def rank_program(g, core, T, topo):
         wt(P, f2)
         f3 = ev(P.matmul(T.bps[:, 0:1], T.ones[:], T.rs[:, 0:1], True, True))
         wt(V, e11, f3)
-        e12 = ev(V.tensor_scalar(T.ci[:, 0:nc], T.cps[:, 0:nc], T.bps[:, 0:1], 0.0, A.add, A.max))
+        e12 = ev(V.tensor_scalar(T.u[:, 0:nc], T.cps[:, 0:nc], T.bps[:, 0:1], LOW, A.add, A.max),
+                 V.tensor_scalar(T.hi[:, 0:nc], T.cps[:, 0:nc], T.bps[:, 0:1], LOW, A.add, A.max))
     else:
         wt(V, e11)
-        e12 = ev(V.tensor_scalar(T.ci[:, 0:nc], T.cps[:, 0:nc], 0.0, None, A.max))
+        e12 = ev(V.tensor_scalar(T.u[:, 0:nc], T.cps[:, 0:nc], LOW, None, A.max),
+                 V.tensor_scalar(T.hi[:, 0:nc], T.cps[:, 0:nc], LOW, None, A.max))
     wt(V, e12)
-    e13 = ev(V.tensor_scalar(T.hl[:, 0:nc], T.ci[:, 0:nc], 4, None, A.arith_shift_right),
-             V.tensor_scalar(T.hl[:, nc:2 * nc], T.ci[:, 0:nc], 15, None, A.bitwise_and))
-    wt(V, e13)
-    e14 = ev(V.tensor_scalar(T.hlf[:, 0:2 * nc], T.hl[:, 0:2 * nc], -1.0, None, A.mult))
-    wt(V, e14, e_t)
-    wt(S, e14, e_t)
+    e13 = ev(V.tensor_tensor(T.nv[:, 0:nc], T.hi[:, 0:nc], T.u[:, 0:nc], A.subtract))
+    wt(V, e_t)
+    wt(S, e13, e_t)
 
     for t in range(0, nc, 2):
         ins = []
-        for u in (t, t + 1):
-            ins.append(V.tensor_scalar(T.oh[:, 128 * u:128 * u + 128], T.nb[:], T.hlf[:, u:u + 1], None, A.is_equal))
-            ins.append(S.activation(T.sg[:, 64 * u:64 * u + 64], T.lt[:], AF.Sign, bias=T.hlf[:, nc + u:nc + u + 1],
-                                    scale=1.0))
+        for j in (t, t + 1):
+            ins.append(V.tensor_scalar(T.oh[:, 128 * j:128 * j + 128], T.nk[:], T.u[:, j:j + 1], None, A.is_gt))
+            ins.append(S.activation(T.sg[:, 64 * j:64 * j + 64], T.lt[:], AF.Sign, bias=T.nv[:, j:j + 1], scale=1.0))
         wt(P, ev(*ins))
-        for u in (t, t + 1):
-            m = P.matmul(T.gps[:, 0:64], T.oh[:, 128 * u:128 * u + 128], T.sg[:, 64 * u:64 * u + 64], u == 0,
-                         u == nc - 1)
+        for j in (t, t + 1):
+            m = P.matmul(T.gps[:, 0:64], T.oh[:, 128 * j:128 * j + 128], T.sg[:, 64 * j:64 * j + 64], j == 0,
+                         j == nc - 1)
     e15 = ev(m)
     wt(V, e15, e7)
     e16 = ev(V.tensor_copy(T.GL[:, 0:64], T.gps[:, 0:64]), V.tensor_copy(T.GL[:, 64:128], T.gps[:, 0:64]))
-    e17 = ev(V.tensor_scalar(T.R2[:], T.UU[:], T.gps[:, 15:16], None, A.mult))
+    e17 = ev(V.tensor_scalar(T.R2[:], T.Am[:], T.gps[:, 15:16], None, A.mult))
     wt(P, e7, e16)
-    P.matmul(T.fps[:, 0:128], T.GL[:], T.hI[:], True, False)
+    P.matmul(T.fps[:, 0:128], T.GL[:], T.Dm[:], True, False)
     wt(P, e17)
     e18 = ev(P.matmul(T.fps[:, 0:128], T.one16[:], T.R2[:], False, True))
     wt(V, e18)
@@ -314,22 +317,12 @@ def rank_program(g, core, T, topo):
     arrived(S)
     wt(S, e19, e_z)
     win = T.xw[:, w0:w1]
-
-    def gat(q, c0, c1):
-        o = T.off[:, c0 // 16:c1 // 16]
-        if q is V:
-            return ev(V.tensor_copy(T.yt[:, c0:c1], win.indirect(o)))
-        return ev(S.activation(T.yt[:, c0:c1], win.indirect(o), AF.Copy))
-
-    g1 = gat(V, 0, 256)
-    g2 = gat(S, 256, 512)
-    g3 = gat(V, 512, 1280)
-    g4 = gat(S, 1280, 2048)
-    for tok, c0, c1 in ((g1, 0, 256), (g2, 256, 512), (g3, 512, 1280)):
+    ends = [0, 320, 1024, 2048]
+    for c0, c1 in zip(ends, ends[1:]):
+        c = (c0 + c1) // 2
+        tok = ev(V.tensor_copy(T.yt[:, c0:c], win.indirect(T.off[:, c0 // 16:c // 16])),
+                 S.activation(T.yt[:, c:c1], win.indirect(T.off[:, c // 16:c1 // 16]), AF.Copy))
         wt(Y, tok)
         Y.dma_start(T.y[:, c0:c1], T.yt[:, c0:c1]).then_inc(T.sem.yst, 16)
-    wt(S, g4)
-    S.dma_start(T.y[:, 1280:2048], T.yt[:, 1280:2048]).then_inc(T.sem.ysc, 16)
-    Y.wait_ge(T.sem.yst, 48)
-    S.wait_ge(T.sem.ysc, 16)
+    Y.wait_ge(T.sem.yst, 16 * (len(ends) - 1))
     g.wait_ge(T.sem.sent, sent[0])

from concourse.bass import DstId, RemoteDMATransfer
from concourse.mybir import AluOpType, ActivationFunctionType, AxisListType

NEV = 64
SCRATCH = {
    "Li": ("sbuf", [128, 32], "int32"),
    "fwi": ("sbuf", [128, 16], "int32"),
    "fwf": ("sbuf", [128, 16], "float32"),
    "rs": ("sbuf", [128, 4], "float32"),
    "Lf": ("sbuf", [128, 32], "float32"),
    "Sc": ("sbuf", [128, 36], "float32"),
    "SB": ("sbuf", [128, 16], "float32"),
    "zz": ("sbuf", [128, 32], "float32"),
    "kc": ("sbuf", [128, 16], "float32"),
    "ni": ("sbuf", [128, 128], "int32"),
    "pi": ("sbuf", [128, 4], "int32"),
    "pj": ("sbuf", [128, 4], "int32"),
    "pf": ("sbuf", [128, 4], "float32"),
    "am": ("sbuf", [128, 128], "int32"),
    "bm": ("sbuf", [128, 128], "int32"),
    "lm": ("sbuf", [128, 64], "int32"),
    "Aeq": ("sbuf", [128, 128], "float32"),
    "Alt": ("sbuf", [128, 128], "float32"),
    "Agt": ("sbuf", [128, 128], "float32"),
    "Ang": ("sbuf", [128, 128], "float32"),
    "Ab": ("sbuf", [128, 128], "float32"),
    "ones": ("sbuf", [128, 128], "float32"),
    "one16": ("sbuf", [128, 128], "float16"),
    "nk": ("sbuf", [128, 128], "bfloat16"),
    "lt": ("sbuf", [128, 64], "bfloat16"),
    "t1": ("sbuf", [128, 128], "float16"),
    "t2": ("sbuf", [128, 128], "float16"),
    "Dm": ("sbuf", [128, 128], "float16"),
    "Am": ("sbuf", [128, 128], "float16"),
    "hi": ("sbuf", [128, 12], "int32"),
    "u": ("sbuf", [128, 12], "float32"),
    "nv": ("sbuf", [128, 12], "float32"),
    "oh": ("sbuf", [128, 1536], "bfloat16"),
    "sg": ("sbuf", [128, 768], "bfloat16"),
    "GL": ("sbuf", [128, 128], "float16"),
    "R2": ("sbuf", [128, 128], "float16"),
    "osb": ("sbuf", [128, 2], "uint16"),
    "off": ("sbuf", [128, 128], "uint16"),
    "xw": ("sbuf", [128, 1540], "float32"),
    "rl": ("sbuf", [128, 256], "float32"),
    "yt": ("sbuf", [128, 2048], "float32"),
    "cps": ("psum", [128, 512], "float32"),
    "bps": ("psum", [128, 512], "float32"),
    "gps": ("psum", [128, 512], "float32"),
    "fps": ("psum", [128, 512], "float32"),
}
SEMAPHORES = (["lnld", "xld", "yst", "sent", "fw", "xm", "xp", "xq", "rla"] + ["l%d" % k for k in range(8)]
              + ["e%d" % k for k in range(NEV)])


def bits(mask):
    return [b for b in range(32) if (mask >> b) & 1]


def tomask(bs):
    m = 0
    for b in bs:
        m |= 1 << b
    return m


def route(T, topo):
    C = T.cores
    n = len(C)
    cut = [r for r in range(n - 1) if topo.chip(C[r]) != topo.chip(C[r + 1])]
    assert len(cut) == 1
    b = cut[0]
    first, second = list(range(b + 1)), list(range(b + 1, n))
    assert topo.may_write(C[b], C[b + 1])
    fwd = [r for r in first if r != b and all(topo.may_write(C[r], C[q]) for q in second)][0]
    cand = [r for r in second if r != b + 1 and topo.may_write(C[r], C[b])]
    near = [r for r in cand if r == b + 2][0]
    far = [r for r in cand if topo.die(C[r]) != topo.die(C[near])][0]
    return b, first, second, fwd, near, far


def rank_program(g, core, T, topo):
    r = T.rank_of(core)
    if r is None:
        return
    C = T.cores
    n = len(C)
    b, first, second, fwd, near, far = route(T, topo)
    mine = first if r in first else second
    A = AluOpType
    AF = ActivationFunctionType
    V, S, P, Y = g.vector, g.scalar, g.tensor, g.sync
    cnt = [0]
    sent = [0]

    def ev(*ins):
        s = T.sem["e%d" % cnt[0]]
        cnt[0] += 1
        for i in ins:
            i.then_inc(s, 1)
        return (s, len(ins))

    def wt(q, *toks):
        for s, v in toks:
            q.wait_ge(s, v)

    onchip = bits(topo.mask(C[mine[0]], C[mine[1]]))
    offchip = bits(topo.mask(C[b], C[b + 1]))
    hi8 = [e for e in onchip if e not in offchip]
    ev8, od8 = onchip[0::2], onchip[1::2]

    def tr(src, dst, sem, ranks, engines):
        ids = [DstId(rid=topo.addr(C[q])[0], pnc=topo.addr(C[q])[1]) for q in ranks]
        sent[0] += len(engines)
        return RemoteDMATransfer(dst_ids=ids, dma_engine_mask=tomask(engines), remote_sem=sem, srcs=[src],
                                 dsts=list(dst))

    def send(*trs):
        g.remote_dma_fused(list(trs), local_sem=T.sem.sent)

    def slot(k, q):
        return 512 * (k - q + 1)

    lists = [k for k in (r - 1, r, r + 1) if 0 <= k < n]
    nc = 4 * len(lists)
    w0 = slot(lists[0], r)
    w1 = slot(lists[-1], r) + 512
    NL = len(offchip)

    def ldests(k):
        grp = first if k in first else second
        d = [q for q in grp if q != k and (q >= k - 1 or (k in first and q == fwd))]
        if k == b:
            d.append(b + 1)
        relay = fwd if k in first else far if k == b + 1 else k
        if relay == k:
            return [d]
        return [[relay], [q for q in d if q != relay]]

    Y.dma_start(T.Li[:, 4 * r:4 * r + 4], T.ln[:]).then_inc(T.sem.lnld, 16)
    xs = slot(r, r)
    S.dma_start(T.xw[:, xs:xs + 512], T.x[:]).then_inc(T.sem.xld, 16)

    e_p = ev(g.iota(T.pi[:, 0:1], [[0, 1]], 0, 1))
    e_n = ev(g.iota(T.ni[:], [[1, 128]], 0, 0))

    g.wait_ge(T.sem.lnld, 16)
    for ld in ldests(r):
        send(tr(T.Li[:, 4 * r:4 * r + 4], [T.Li[:, 4 * r:4 * r + 4] for q in ld], T.sem["l%d" % r], ld, offchip))

    g.wait_ge(T.sem.xld, 16)
    xall = T.xw[:, xs:xs + 512]

    def xdst(q):
        s = slot(r, q)
        return T.xw[:, s:s + 512]

    def xsend(k):
        if k == b:
            return [(b + 1, offchip), (k - 1, hi8)]
        if k == b + 1:
            return []
        q2 = [q for q in (k - 1, k + 1) if 0 <= q < n]
        pool = hi8 if k in (fwd, near, far) else onchip
        if len(q2) == 1:
            return [(q2[0], pool)]
        return [(q2[0], pool[0::2]), (q2[1], pool[1::2])]

    nx = {}
    for k in range(n):
        for q, e in xsend(k):
            nx[(k, q)] = len(e)
    if r == b + 1:
        s = slot(r, near)
        send(tr(T.xw[:, xs:xs + 256], [T.xw[:, s:s + 256]], T.sem.xm, [near], od8),
             tr(T.xw[:, xs + 256:xs + 512], [T.rl[:]], T.sem.rla, [far], ev8))
        send(tr(T.xw[:, xs + 256:xs + 512], [T.xw[:, s + 256:s + 512]], T.sem.xq, [near], od8))
    else:
        send(*[tr(xall, [xdst(q)], T.sem.xm if q > r else T.sem.xp, [q], e) for q, e in xsend(r)])

    if r == fwd:
        for k in first:
            if k != r:
                g.wait_ge(T.sem["l%d" % k], NL)
        m = 4 * len(first)
        send(tr(T.Li[:, 0:m], [T.fwi[:, 0:m] for q in second], T.sem.fw, second, offchip))
    if r == far:
        k = b + 1
        g.wait_ge(T.sem["l%d" % k], NL)
        send(tr(T.Li[:, 4 * k:4 * k + 4], [T.Li[:, 4 * k:4 * k + 4]], T.sem["l%d" % k], [b], offchip))
        g.wait_ge(T.sem.rla, len(ev8))
        s = slot(k, b)
        send(tr(T.rl[:], [T.xw[:, s + 256:s + 512]], T.sem.xq, [b], offchip))
    if r == near:
        k = b + 1
        g.wait_ge(T.sem.xm, len(od8))
        s, s0 = slot(k, b), slot(k, r)
        send(tr(T.xw[:, s0:s0 + 256], [T.xw[:, s:s + 256]], T.sem.xp, [b], offchip))

    LOW = -15.0 / 32
    e_m = ev(V.memset(T.kc[:], (LOW - 128 * r) / 8), V.memset(T.ones[:], 1.0 / 16))
    zero = [V.memset(T.Sc[:], 0.0), V.memset(T.zz[:], 0.0)]
    if r >= n - 2:
        zero.append(V.memset(T.xw[:, w1:w1 + 4], 0.0))
        w1 += 1
    e_z = ev(*zero)
    wt(V, e_p, e_n)
    e1 = ev(V.tensor_scalar(T.pj[:, 0:1], T.pi[:, 0:1], 7, None, A.bitwise_and),
            V.tensor_scalar(T.pj[:, 1:2], T.pi[:, 0:1], 3, None, A.arith_shift_right),
            V.tensor_scalar(T.pj[:, 2:3], T.pi[:, 0:1], 12, None, A.bitwise_and),
            V.tensor_copy(T.pf[:, 3:4], T.pi[:, 0:1]),
            V.tensor_scalar(T.pf[:, 2:3], T.pi[:, 0:1], 1.0, None, A.add),
            V.tensor_scalar(T.am[:], T.ni[:], 7, None, A.bitwise_and),
            V.tensor_scalar(T.bm[:], T.ni[:], 3, None, A.arith_shift_right),
            V.tensor_scalar(T.lm[:], T.ni[:, 0:64], 15, None, A.bitwise_and))
    i_nk = V.tensor_scalar(T.nk[:], T.ni[:], 0.5, None, A.add)
    wt(V, e1, e_z, e_m)
    base_lists = [k for k in mine if k < lists[0] and not (r in second and k in first)]
    scan_lists = base_lists + lists
    e0 = 4 * len(base_lists)
    e2 = ev(V.tensor_copy(T.pf[:, 0:2], T.pj[:, 0:2]),
            V.tensor_scalar(T.osb[:, 0:1], T.pj[:, 2:3], float(e0), None, A.add))
    e_t = ev(i_nk, V.tensor_scalar(T.lt[:], T.lm[:], -7.0, 1.0 / 16, A.add, A.mult))
    wt(V, e2)
    e3 = ev(V.tensor_scalar(T.Aeq[:], T.am[:], T.pf[:, 0:1], 1.0 / 16, A.is_equal, A.mult),
            V.tensor_scalar(T.Ab[:], T.bm[:], T.pf[:, 1:2], -1.0, A.is_lt, A.mult))
    e4 = ev(V.tensor_scalar(T.Alt[:], T.am[:], T.pf[:, 0:1], 1.0 / 16, A.is_gt, A.mult),
            V.tensor_scalar(T.Agt[:], T.am[:], T.pf[:, 0:1], 1.0 / 16, A.is_lt, A.mult))
    wt(V, e3)
    e5 = ev(V.tensor_tensor(T.Ang[:], T.Ab[:], T.Aeq[:], A.mult))
    e6 = ev(V.tensor_scalar(T.t1[:], T.ni[:], T.pf[:, 3:4], 0.5, A.is_equal, A.mult),
            V.tensor_scalar(T.t2[:], T.ni[:], T.pf[:, 2:3], 0.5, A.is_equal, A.mult))
    wt(V, e6)
    e7 = ev(V.tensor_tensor(T.Dm[:], T.t1[:], T.t2[:], A.subtract),
            V.tensor_tensor(T.Am[:], T.t1[:], T.t2[:], A.add),
            V.memset(T.zz[:], 0.0) if False else V.tensor_scalar(T.one16[:], T.ones[:], 16.0, None, A.mult))

    wt(P, e_m)
    P.matmul(T.cps[:, 0:nc], T.ones[:], T.kc[:, 0:nc], True, False)
    k0, k1 = scan_lists[0], scan_lists[-1]
    V.wait_ge(T.sem.lnld, 16)
    for k in scan_lists:
        if k != r:
            V.wait_ge(T.sem["l%d" % k], NL)
    ns = 4 * len(scan_lists)
    e8 = ev(V.tensor_copy(T.Lf[:, 0:ns], T.Li[:, 4 * k0:4 * k1 + 4]))
    wt(V, e8)
    e9 = ev(V.tensor_tensor_scan(T.Sc[:, 1:1 + ns], T.zz[:, 0:ns], T.Lf[:, 0:ns], 0.0, A.add, A.add))
    wt(V, e9)
    e10 = ev(V.tensor_copy(T.SB[:], T.Sc[:].indirect(T.osb[:, 0:1])))
    wt(P, e5, e8)
    P.matmul(T.cps[:, 0:nc], T.Ang[:], T.Lf[:, e0:e0 + nc], False, False)
    wt(P, e3, e9)
    P.matmul(T.cps[:, 0:nc], T.Aeq[:], T.Sc[:, e0 + 1:e0 + 1 + nc], False, False)
    wt(P, e4, e10)
    P.matmul(T.cps[:, 0:nc], T.Alt[:], T.SB[:, 4:4 + nc], False, False)
    e11 = ev(P.matmul(T.cps[:, 0:nc], T.Agt[:], T.SB[:, 0:nc], False, True))

    if r in second:
        nf = 4 * len([k for k in first if k < lists[0]])
        V.wait_ge(T.sem.fw, NL)
        f1 = ev(V.tensor_copy(T.fwf[:, 0:nf], T.fwi[:, 0:nf]))
        wt(V, f1)
        f2 = ev(V.tensor_reduce(T.rs[:, 0:1], T.fwf[:, 0:nf], AxisListType.X, A.add))
        wt(P, f2)
        f3 = ev(P.matmul(T.bps[:, 0:1], T.ones[:], T.rs[:, 0:1], True, True))
        wt(V, e11, f3)
        e12 = ev(V.tensor_scalar(T.u[:, 0:nc], T.cps[:, 0:nc], T.bps[:, 0:1], LOW, A.add, A.max),
                 V.tensor_scalar(T.hi[:, 0:nc], T.cps[:, 0:nc], T.bps[:, 0:1], LOW, A.add, A.max))
    else:
        wt(V, e11)
        e12 = ev(V.tensor_scalar(T.u[:, 0:nc], T.cps[:, 0:nc], LOW, None, A.max),
                 V.tensor_scalar(T.hi[:, 0:nc], T.cps[:, 0:nc], LOW, None, A.max))
    wt(V, e12)
    e13 = ev(V.tensor_tensor(T.nv[:, 0:nc], T.hi[:, 0:nc], T.u[:, 0:nc], A.subtract))
    wt(V, e_t)
    wt(S, e13, e_t)

    for t in range(0, nc, 2):
        ins = []
        for j in (t, t + 1):
            ins.append(V.tensor_scalar(T.oh[:, 128 * j:128 * j + 128], T.nk[:], T.u[:, j:j + 1], None, A.is_gt))
            ins.append(S.activation(T.sg[:, 64 * j:64 * j + 64], T.lt[:], AF.Sign, bias=T.nv[:, j:j + 1], scale=1.0))
        wt(P, ev(*ins))
        for j in (t, t + 1):
            m = P.matmul(T.gps[:, 0:64], T.oh[:, 128 * j:128 * j + 128], T.sg[:, 64 * j:64 * j + 64], j == 0,
                         j == nc - 1)
    e15 = ev(m)
    wt(V, e15, e7)
    e16 = ev(V.tensor_copy(T.GL[:, 0:64], T.gps[:, 0:64]), V.tensor_copy(T.GL[:, 64:128], T.gps[:, 0:64]))
    e17 = ev(V.tensor_scalar(T.R2[:], T.Am[:], T.gps[:, 15:16], None, A.mult))
    wt(P, e7, e16)
    P.matmul(T.fps[:, 0:128], T.GL[:], T.Dm[:], True, False)
    wt(P, e17)
    e18 = ev(P.matmul(T.fps[:, 0:128], T.one16[:], T.R2[:], False, True))
    wt(V, e18)
    e19 = ev(V.tensor_copy(T.off[:], T.fps[:, 0:128]))

    def arrived(q):
        q.wait_ge(T.sem.xld, 16)
        for k in lists:
            if k == r:
                continue
            if k == b + 1 and r == near:
                q.wait_ge(T.sem.xm, len(od8))
                q.wait_ge(T.sem.xq, len(od8))
            elif k == b + 1 and r == b:
                q.wait_ge(T.sem.xp, len(offchip))
                q.wait_ge(T.sem.xq, len(offchip))
            elif k < r:
                q.wait_ge(T.sem.xm, nx[(k, r)])
            else:
                q.wait_ge(T.sem.xp, nx[(k, r)])

    arrived(V)
    wt(V, e19)
    arrived(S)
    wt(S, e19, e_z)
    win = T.xw[:, w0:w1]
    ends = [0, 320, 1024, 2048]
    for c0, c1 in zip(ends, ends[1:]):
        c = (c0 + c1) // 2
        tok = ev(V.tensor_copy(T.yt[:, c0:c], win.indirect(T.off[:, c0 // 16:c // 16])),
                 S.activation(T.yt[:, c:c1], win.indirect(T.off[:, c // 16:c1 // 16]), AF.Copy))
        wt(Y, tok)
        Y.dma_start(T.y[:, c0:c1], T.yt[:, c0:c1]).then_inc(T.sem.yst, 16)
    Y.wait_ge(T.sem.yst, 16 * (len(ends) - 1))
    g.wait_ge(T.sem.sent, sent[0])
